import numpy as np
import ml_dtypes


def mxq(x, axis, fmt="e4m3"):
    dtype, down = {"e4m3": (ml_dtypes.float8_e4m3fn, 7), "e5m2": (ml_dtypes.float8_e5m2, 14)}[fmt]
    v = np.moveaxis(np.asarray(x, np.float32).astype(ml_dtypes.bfloat16).astype(np.float64), axis, -1)
    blocks = v.reshape(v.shape[:-1] + (-1, 32))
    amax = np.abs(blocks).max(-1, keepdims=True)
    byte = np.maximum(np.where(amax > 0, np.frexp(amax)[1] - 1 + 127, 0) - down, 1)
    scale = np.exp2(byte - 127.0)
    codes = (blocks / scale).astype(np.float32).astype(dtype).astype(np.float64)
    return np.moveaxis((codes * scale).reshape(v.shape), -1, axis)


WIDE = False


def mx_kscale(k):
    if not WIDE:
        return np.ones(k)
    levels = np.array([10, -10, 5, -5, 0])
    if k % 512:
        return np.exp2(np.random.permutation(np.resize(levels, k // 32))).repeat(32)
    a = np.empty((k // 512, 16))
    for p in range(k // 512):
        a[p, :8] = np.random.permutation(np.resize(levels, 8))
        for g in range(8):
            far = levels[np.abs(levels - a[p, g]) >= 10]
            a[p, g + 8] = far[np.random.randint(len(far))]
    return np.exp2(a.ravel()).repeat(32)


def f64(x):
    return np.asarray(x).astype(np.float64)


def striped(idx):
    return np.tile(idx.reshape(-1, 16).T, (8, 1)).astype(np.uint16)


def unstriped(offs):
    return offs[:16].T.reshape(-1).astype(np.int64)


def striped8(idx):
    return np.concatenate([x.reshape(-1, 16).T for x in idx]).astype(np.uint16)


def runs(offs, k):
    lists = np.stack([offs[16 * r : 16 * r + 16].T.reshape(-1) for r in range(8)]).astype(np.int64)
    return lists[np.arange(k) % 512 // 64]


def pack_weight(w):
    k, n = w.shape
    w = f64(np.asarray(w, np.float32).astype(ml_dtypes.bfloat16)).reshape(k // 32, 32, n)
    amax = np.abs(w).max(1)
    byte = np.clip(np.where(amax > 0, np.frexp(amax)[1] - 1 + 127 - 7, 1), 1, 254)
    scaled = (w * np.exp2(127.0 - byte)[:, None, :]).reshape(k, n).astype(np.float32)
    words = np.ascontiguousarray(scaled.reshape(k // 512, 128, 4, n).transpose(0, 1, 3, 2)).astype(ml_dtypes.float8_e4m3fn).view(np.uint8)
    return words, np.ascontiguousarray(byte.astype(np.uint8).reshape(k // 512, 16, n))


def unpack_weight(words, scales):
    g, p, n, _ = words.shape
    vals = np.ascontiguousarray(words).view(ml_dtypes.float8_e4m3fn).astype(np.float64) * np.repeat(np.exp2(scales.astype(np.float64) - 127.0), 8, axis=1)[..., None]
    return vals.transpose(0, 1, 3, 2).reshape(g * 512, n)


K, T, S, V, H, W = 512, 2048, 512, 512, 512, 2048


def setup_inputs():
    n = np.random.standard_normal
    s = mx_kscale(K)[:, None]
    u = mx_kscale(S)
    packed_xT = pack_weight(n((K, T)) * s)
    return {
        "x_words": packed_xT[0],
        "x_scales": packed_xT[1],
        "w1": (n((K, H)) / np.sqrt(K) / s).astype(np.float32),
        "w2": (n((K, H)) / np.sqrt(K) / s).astype(np.float32),
        "ga": (np.random.uniform(0.5, 1.5, (H, 1)) * u[:, None]).astype(np.float32),
        "gb": (np.random.uniform(0.5, 1.5, (H, 1)) / u[:, None]).astype(np.float32),
        "offs": striped(np.random.permutation(T)[:S]),
        "two": striped(np.random.permutation(T)[:V]),
        "n1": striped(np.random.randint(0, S, W)),
        "n2": striped8(np.stack([np.random.permutation(V) for _ in range(8)])),
        "n3": striped8(np.stack([np.random.permutation(V) for _ in range(8)])),
        "n4": striped(np.random.permutation(V)),
        "n5": striped(np.random.permutation(V)),
    }


def reference(x_words, x_scales, w1, w2, ga, gb, offs, two, n1, n2, n3, n4, n5):
    xq = unpack_weight(x_words, x_scales)[:, unstriped(offs)]
    a = mxq(f64(w1), 0, "e4m3").T @ xq
    mb = a[:, unstriped(n1)]
    sq = (mb) ** 2
    qs = sq.reshape(H, S, 4).sum(axis=2)
    z = f64(ga) * (a / np.sqrt(qs + 0.5))
    x_two = unpack_weight(x_words, x_scales)[:, unstriped(two)]
    b = mxq(f64(w2), 0, "e4m3").T @ x_two
    z2 = f64(gb) * ((b[np.arange(H)[:, None], runs(n2, H)]) / (np.abs(b) + np.abs(b[np.arange(H)[:, None], runs(n3, H)]) + 0.5))
    s = 0.0625 * ((mxq(z, 0, "e4m3").T @ mxq(z2, 0, "e4m3")))
    st = s + s[:, unstriped(n4)]
    return st * (np.tanh(st[:, unstriped(n5)]))

@@ -1,0 +1,251 @@
+from contextlib import ExitStack
+
+import concourse.mybir as mybir
+from concourse.masks import make_identity
+
+F32 = mybir.dt.float32
+BF16 = mybir.dt.bfloat16
+I32 = mybir.dt.int32
+U32 = mybir.dt.uint32
+U16 = mybir.dt.uint16
+U8 = mybir.dt.uint8
+FP8X4 = mybir.dt.float8_e4m3fn_x4
+ALU = mybir.AluOpType
+ACT = mybir.ActivationFunctionType
+
+P = 128
+PACK = 4
+T = 2048
+N = 512
+HALF = N // 2
+SPARE = 16
+FLOPS = 3 * 2 * 512 * 512 * 512
+
+
+def tile_picked_kqgvarnorm2hopp_none_p_kernel(tc, x_words, x_scales, w1, w2, ga, gb, offs, two, n1, n2, n3, n4, n5, out):
+    nc = tc.nc
+    with ExitStack() as ctx:
+        keep = ctx.enter_context(tc.tile_pool(name="keep", bufs=1))
+        ring = ctx.enter_context(tc.tile_pool(name="ring", bufs=2))
+        reuse = ctx.enter_context(tc.tile_pool(name="reuse", bufs=1))
+        psum = ctx.enter_context(tc.psum_pool(name="psum", bufs=1))
+
+        def load_list(src, name):
+            t = keep.tile(list(src.shape), U16, name=name)
+            nc.sync.dma_start(t[:], src)
+            return t
+
+        def load_weight(w, name):
+            raw = keep.tile([P, PACK, N], F32, name=name)
+            nc.sync.dma_start(raw[:], w.rearrange("(p j) c -> p j c", j=PACK))
+            return raw
+
+        def load_gain(g, name):
+            t = keep.tile([P, PACK], F32, name=name)
+            nc.sync.dma_start(t[:], g.rearrange("(p t) o -> p (t o)", t=PACK))
+            return t
+
+        def half(lst, h):
+            return lst[:, 16 * h : 16 * (h + 1)]
+
+        def cols(h):
+            return slice(HALF * h, HALF * (h + 1))
+
+        xs_rows = keep.tile([P, T // 4], I32, name="xs_rows")
+        for q in range(4):
+            nc.sync.dma_start(xs_rows[32 * q : 32 * q + 4, :], x_scales[0, 4 * q : 4 * q + 4, :].bitcast(I32))
+        two_l = load_list(two, "two_l")
+        offs_l = load_list(offs, "offs_l")
+        w2_raw = load_weight(w2, "w2_raw")
+        xw = keep.tile([P, T], U32, name="xw")
+        nc.sync.dma_start(xw[:].bitcast(I32), x_words[0].rearrange("p n t -> p (n t)").bitcast(I32))
+        n3_l = load_list(n3, "n3_l")
+        gb_sb = load_gain(gb, "gb_sb")
+        w1_raw = load_weight(w1, "w1_raw")
+        ga_sb = load_gain(ga, "ga_sb")
+        n1_l = load_list(n1, "n1_l")
+        n2_l = load_list(n2, "n2_l")
+        n4_l = load_list(n4, "n4_l")
+        n5_l = load_list(n5, "n5_l")
+
+        xs = keep.tile([P, T], U8, name="xs")
+        nc.vector.memset(xs[:].bitcast(I32), 0)
+        asq = [keep.tile([P, N + SPARE], F32, name=f"asq{t}") for t in range(PACK)]
+        for t in range(PACK):
+            nc.gpsimd.memset(asq[t][:, N:], 0.0)
+        ident = keep.tile([P, P], F32, name="ident")
+        make_identity(nc, ident[:])
+
+        def mx_tiles(name):
+            return (
+                keep.tile([P, N], U32, name=name + "_codes", align_bytes=64),
+                keep.tile([P, N], U8, name=name + "_scales", align_bytes=64),
+            )
+
+        def quantize(dst, src, c):
+            nc.vector.quantize_mx(out=dst[0][:, c].bitcast(FP8X4), scales=dst[1][:, c], in_=src)
+
+        def matmul(acc, lhs, c, rhs):
+            nc.tensor.matmul_mx(out=acc[:], lhsT=lhs[0][:, c].bitcast(FP8X4), lhsT_scale=lhs[1][:, c],
+                                rhs=rhs[0][:].bitcast(FP8X4), rhs_scale=rhs[1][:], start=True, stop=True)
+
+        def cast_weight(shares, raw, grouped):
+            dst = grouped[:].rearrange("p (t m j) -> p m j t", t=PACK, j=PACK)
+            src = raw[:].rearrange("p j (m t) -> p m j t", t=PACK)
+            for copy, ms in shares:
+                copy(dst[:, ms], src[:, ms])
+
+        def safe_inverse(g, name):
+            safe = keep.tile([P, PACK], F32, name=name + "_safe")
+            nc.vector.scalar_tensor_tensor(safe[:], g[:], 0.0, g[:], ALU.is_equal, ALU.add)
+            inv = keep.tile([P, PACK], F32, name=name + "_inv")
+            nc.vector.reciprocal(inv[:], safe[:])
+            return inv
+
+        def interleaved_product(dst, in0, in1):
+            nc.vector.tensor_tensor(
+                dst.rearrange("p (c i t) -> p c t i", i=2, t=PACK),
+                in0.rearrange("p t (c i) -> p c t i", i=2),
+                in1.rearrange("p t (c i) -> p c t i", i=2),
+                ALU.mult,
+            )
+
+        w2g = reuse.tile([P, PACK * N], BF16, name="w2g", align_bytes=64, offset=0)
+        w1g = keep.tile([P, PACK * N], BF16, name="w1g", align_bytes=64)
+        x_two, x_offs = [
+            (
+                reuse.tile([P, N], U32, name=name + "_codes", align_bytes=64, offset=4 * N * i),
+                keep.tile([P, N], U8, name=name + "_scales", align_bytes=64),
+            )
+            for i, name in enumerate(("x_two", "x_offs"))
+        ]
+        w1q, w2q = mx_tiles("w1q"), mx_tiles("w2q")
+        zq, z2q = mx_tiles("zq"), mx_tiles("z2q")
+        whole = slice(0, N)
+
+        for q in range(4):
+            nc.vector.tensor_copy(xs[32 * q : 32 * q + 4, :].bitcast(I32), xs_rows[32 * q : 32 * q + 4, :])
+        nc.vector.tensor_copy(x_two[1][:], xs[:].indirect(two_l[:]))
+        nc.vector.tensor_copy(x_offs[1][:], xs[:].indirect(offs_l[:]))
+        cast_weight([(nc.scalar.copy, slice(0, 96)), (nc.vector.tensor_copy, slice(96, P))], w2_raw, w2g)
+        quantize(w2q, w2g[:], whole)
+        nc.vector.tensor_copy(x_two[0][:], xw[:].indirect(two_l[:]))
+        b_ps = [psum.tile([P, N], F32, name=f"b_ps{t}", tag=f"bank{t}") for t in range(PACK)]
+        for t in range(PACK):
+            matmul(b_ps[t], w2q, slice(P * t, P * (t + 1)), x_two)
+
+        babs = [keep.tile([P, N], F32, name=f"babs{t}") for t in range(PACK)]
+        bg = [keep.tile([P, N], F32, name=f"bg{t}") for t in range(PACK)]
+        g3 = keep.tile([P, PACK, N], F32, name="g3")
+        den = keep.tile([P, PACK, N], F32, name="den")
+        rb = keep.tile([P, PACK, N], F32, name="rb")
+        u = keep.tile([P, PACK, N], F32, name="u")
+        aga = keep.tile([P, PACK, N], F32, name="aga")
+        qs = keep.tile([P, PACK, N], F32, name="qs")
+        z2g = keep.tile([P, PACK * N], BF16, name="z2g", align_bytes=64)
+        st = [keep.tile([P, 2 * N], F32, name=f"st{m}") for m in range(4)]
+        sums = {}
+
+        def scale_b(t):
+            nc.vector.tensor_scalar(bg[t][:], b_ps[t][:], gb_sb[:, t : t + 1], None, ALU.mult)
+
+        def fetch_n3(t):
+            for h in range(2):
+                nc.scalar.activation(g3[:, t, cols(h)], babs[t][:].indirect(half(n3_l, h)), ACT.Copy)
+            nc.gpsimd.tensor_tensor(den[:, t, :], g3[:, t, :], babs[t][:], ALU.add)
+
+        def root_b(t):
+            nc.scalar.activation(rb[:, t, :], den[:, t, :], ACT.Abs_reciprocal_sqrt, bias=0.5, scale=gb_abs_inv[:, t : t + 1])
+
+        def fetch_n2(t):
+            for h in range(2):
+                nc.vector.tensor_tensor(u[:, t, cols(h)], bg[t][:].indirect(half(n2_l, h)), rb[:, t, cols(h)], ALU.mult)
+
+        def members(m, t):
+            if t == 0:
+                sums[m] = psum.tile([P, PACK, P], F32, name="sums", tag=f"bank{2 + m % 2}")
+            g = ring.tile([P, N], F32, name="g", bufs=4)
+            nc.scalar.activation(g[:], asq[t][:].indirect(n1_l[:, 32 * m : 32 * (m + 1)]), ACT.Copy)
+            gv = g[:].rearrange("p (j r) -> p r j", r=4)
+            for r in range(4):
+                nc.tensor.matmul(sums[m][:, t, :], gv[:, r, :], ident[:], start=(r == 0), stop=(r == 3), is_transpose=True)
+
+        roots = {}
+
+        def root_a(m):
+            blk = slice(P * m, P * (m + 1))
+            nc.scalar.activation(qs[:, :, blk], sums[m][:], ACT.Abs_reciprocal_sqrt, bias=0.5)
+            roots[m] = psum.tile([P, PACK, P], F32, name="rs", tag=f"bank{m % 2}")
+            for t in range(PACK):
+                nc.tensor.transpose(roots[m][:, t, :], qs[:, t, blk], ident[:])
+
+        def finish_block(m):
+            blk = slice(P * m, P * (m + 1))
+            zg = ring.tile([P, PACK * P], BF16, name="zg", align_bytes=64)
+            interleaved_product(zg[:], roots[m][:], aga[:, :, blk])
+            quantize(zq, zg[:], blk)
+            s_ps = psum.tile([P, N], F32, name="s_ps", tag=f"bank{PACK + m}")
+            matmul(s_ps, zq, blk, z2q)
+            s2 = st[m][:, N:]
+            nc.vector.tensor_scalar(s2, s_ps[:], 0.125, None, ALU.mult)
+            g4 = ring.tile([P, N], F32, name="g4")
+            for h in range(2):
+                nc.vector.tensor_copy(g4[:, cols(h)], s2.indirect(half(n4_l, h)))
+            if m < 3:
+                nc.gpsimd.tensor_tensor(st[m][:, :N], s2, g4[:], ALU.add)
+            else:
+                nc.vector.scalar_tensor_tensor(st[m][:, :N], s_ps[:], 0.125, g4[:], ALU.mult, ALU.add)
+
+        for t in range(2):
+            nc.scalar.activation(babs[t][:], b_ps[t][:], ACT.Abs, scale=gb_sb[:, t : t + 1])
+            fetch_n3(t)
+
+        nc.vector.tensor_copy(x_offs[0][:], xw[:].indirect(offs_l[:]))
+        cast_weight([(nc.vector.tensor_copy, slice(0, P))], w1_raw, w1g)
+        gb_neg = keep.tile([P, PACK], F32, name="gb_neg")
+        nc.vector.tensor_scalar(gb_neg[:], gb_sb[:], -1.0, None, ALU.mult)
+        quantize(w1q, w1g[:], whole)
+        a_ps = [psum.tile([P, N], F32, name=f"a_ps{t}", tag=f"bank{PACK + t}") for t in range(PACK)]
+        for t in range(PACK):
+            matmul(a_ps[t], w1q, slice(P * t, P * (t + 1)), x_offs)
+        gb_inv = safe_inverse(gb_sb, "gb")
+        gb_abs_inv = keep.tile([P, PACK], F32, name="gb_abs_inv")
+        nc.vector.scalar_tensor_tensor(gb_abs_inv[:], gb_inv[:], -1.0, gb_inv[:], ALU.mult, ALU.max)
+        ga_inv = safe_inverse(ga_sb, "ga")
+
+        for t in range(2, PACK):
+            scale_b(t)
+            nc.vector.scalar_tensor_tensor(babs[t][:], b_ps[t][:], gb_neg[:, t : t + 1], bg[t][:], ALU.mult, ALU.max)
+            fetch_n3(t)
+        for t in range(PACK):
+            col = slice(t, t + 1)
+            nc.vector.tensor_scalar(aga[:, t, :], a_ps[t][:], ga_sb[:, col], None, ALU.mult)
+            nc.vector.scalar_tensor_tensor(asq[t][:, :N], aga[:, t, :], ga_inv[:, col], a_ps[t][:], ALU.mult, ALU.mult)
+            root_b(t)
+            members(0, t)
+        for t in range(2):
+            scale_b(t)
+        for t in range(PACK):
+            fetch_n2(t)
+            members(1, t)
+            if t == 1:
+                root_a(0)
+        for h in range(2):
+            interleaved_product(z2g[:, PACK * HALF * h : PACK * HALF * (h + 1)], u[:, :, cols(h)], rb[:, :, cols(h)])
+        quantize(z2q, z2g[:], whole)
+        finish_block(0)
+        for m in range(2, 4):
+            for t in range(PACK):
+                members(m, t)
+                if t == 1:
+                    root_a(m - 1)
+                    finish_block(m - 1)
+        root_a(3)
+        finish_block(3)
+
+        for m in range(4):
+            for c, lst in ([(cols(h), half(n5_l, h)) for h in range(2)] if m == 3 else [(whole, n5_l[:])]):
+                nc.scalar.activation(qs[:, m, c], st[m][:].indirect(lst), ACT.Sigmoid)
+                o = ring.tile([P, N], F32, name="o", bufs=5)
+                nc.vector.scalar_tensor_tensor(o[:, c], qs[:, m, c], 0.5, st[m][:, c], ALU.subtract, ALU.mult)
+                nc.sync.dma_start(out[P * m : P * (m + 1), c], o[:, c])

@@ -51,6 +51,9 @@ def tile_picked_kqgvarnorm2hopp_none_p_kernel(tc, x_words, x_scales, w1, w2, ga,
         def cols(h):
             return slice(HALF * h, HALF * (h + 1))
 
+        warm = keep.tile([P, 2], F32, name="warm")
+        nc.gpsimd.memset(warm[:, 0:1], 1.0)
+        nc.scalar.activation(warm[:, 1:2], warm[:, 0:1], ACT.Abs_reciprocal_sqrt)
         xs_rows = keep.tile([P, T // 4], I32, name="xs_rows")
         for q in range(4):
             nc.sync.dma_start(xs_rows[32 * q : 32 * q + 4, :], x_scales[0, 4 * q : 4 * q + 4, :].bitcast(I32))
@@ -60,8 +63,8 @@ def tile_picked_kqgvarnorm2hopp_none_p_kernel(tc, x_words, x_scales, w1, w2, ga,
         xw = keep.tile([P, T], U32, name="xw")
         nc.sync.dma_start(xw[:].bitcast(I32), x_words[0].rearrange("p n t -> p (n t)").bitcast(I32))
         n3_l = load_list(n3, "n3_l")
-        gb_sb = load_gain(gb, "gb_sb")
         w1_raw = load_weight(w1, "w1_raw")
+        gb_sb = load_gain(gb, "gb_sb")
         ga_sb = load_gain(ga, "ga_sb")
         n1_l = load_list(n1, "n1_l")
         n2_l = load_list(n2, "n2_l")
@@ -70,9 +73,7 @@ def tile_picked_kqgvarnorm2hopp_none_p_kernel(tc, x_words, x_scales, w1, w2, ga,
 
         xs = keep.tile([P, T], U8, name="xs")
         nc.vector.memset(xs[:].bitcast(I32), 0)
-        asq = [keep.tile([P, N + SPARE], F32, name=f"asq{t}") for t in range(PACK)]
-        for t in range(PACK):
-            nc.gpsimd.memset(asq[t][:, N:], 0.0)
+        asq = [keep.tile([P, 2 * N], F32, name=f"asq{t}") for t in range(PACK)]
         ident = keep.tile([P, P], F32, name="ident")
         make_identity(nc, ident[:])
 
@@ -137,7 +138,6 @@ def tile_picked_kqgvarnorm2hopp_none_p_kernel(tc, x_words, x_scales, w1, w2, ga,
         babs = [keep.tile([P, N], F32, name=f"babs{t}") for t in range(PACK)]
         bg = [keep.tile([P, N], F32, name=f"bg{t}") for t in range(PACK)]
         g3 = keep.tile([P, PACK, N], F32, name="g3")
-        den = keep.tile([P, PACK, N], F32, name="den")
         rb = keep.tile([P, PACK, N], F32, name="rb")
         u = keep.tile([P, PACK, N], F32, name="u")
         aga = keep.tile([P, PACK, N], F32, name="aga")
@@ -152,28 +152,49 @@ def tile_picked_kqgvarnorm2hopp_none_p_kernel(tc, x_words, x_scales, w1, w2, ga,
         def fetch_n3(t):
             for h in range(2):
                 nc.scalar.activation(g3[:, t, cols(h)], babs[t][:].indirect(half(n3_l, h)), ACT.Copy)
-            nc.gpsimd.tensor_tensor(den[:, t, :], g3[:, t, :], babs[t][:], ALU.add)
+            nc.gpsimd.tensor_tensor(asq[t][:, N:], g3[:, t, :], babs[t][:], ALU.add)
 
         def root_b(t):
-            nc.scalar.activation(rb[:, t, :], den[:, t, :], ACT.Abs_reciprocal_sqrt, bias=0.5, scale=gb_abs_inv[:, t : t + 1])
+            nc.scalar.activation(rb[:, t, :], asq[t][:, N:], ACT.Abs_reciprocal_sqrt, bias=0.5, scale=(1.0 if t < 2 else gb_abs_inv[:, t : t + 1]))
 
         def fetch_n2(t):
             for h in range(2):
                 nc.vector.tensor_tensor(u[:, t, cols(h)], bg[t][:].indirect(half(n2_l, h)), rb[:, t, cols(h)], ALU.mult)
 
+        modes = ["pe4","pair","pair","v"]
+
         def members(m, t):
-            if t == 0:
+            mode = modes[m]
+            if mode == "mix":
+                mode = "pe4" if t < 2 else "pair"
+            if t == 0 and mode != "v":
                 sums[m] = psum.tile([P, PACK, P], F32, name="sums", tag=f"bank{2 + m % 2}")
-            g = ring.tile([P, N], F32, name="g", bufs=4)
+            if False:
+                g = keep.tile([P, N], F32, name="g", tag=f"zg{m % 2}", align_bytes=64)
+            else:
+                g = ring.tile([P, N], F32, name="g", bufs=6)
             nc.scalar.activation(g[:], asq[t][:].indirect(n1_l[:, 32 * m : 32 * (m + 1)]), ACT.Copy)
+            if mode == "v":
+                nc.vector.tensor_reduce(qs[:, t, P * m : P * (m + 1)], g[:].rearrange("p (j r) -> p j r", r=4), mybir.AxisListType.X, ALU.add)
+                return
             gv = g[:].rearrange("p (j r) -> p r j", r=4)
-            for r in range(4):
-                nc.tensor.matmul(sums[m][:, t, :], gv[:, r, :], ident[:], start=(r == 0), stop=(r == 3), is_transpose=True)
+            if mode == "pair":
+                pairs = ring.tile([P, 2, P], F32, name="pairs", bufs=4)
+                gj = g[:].rearrange("p (j r) -> p j r", r=4)
+                nc.vector.tensor_tensor(pairs[:].rearrange("p r j -> p j r"), gj[:, :, 0:2], gj[:, :, 2:4], ALU.add)
+                gv = pairs[:]
+            terms = gv.shape[1]
+            for r in range(terms):
+                nc.tensor.matmul(sums[m][:, t, :], gv[:, r, :], ident[:], start=(r == 0), stop=(r == terms - 1), is_transpose=True)
 
         roots = {}
 
         def root_a(m):
             blk = slice(P * m, P * (m + 1))
+            if modes[m] == "v":
+                roots[m] = keep.tile([P, PACK, P], F32, name="rs_sb")
+                nc.scalar.activation(roots[m][:], qs[:, :, blk], ACT.Abs_reciprocal_sqrt, bias=0.5)
+                return
             nc.scalar.activation(qs[:, :, blk], sums[m][:], ACT.Abs_reciprocal_sqrt, bias=0.5)
             roots[m] = psum.tile([P, PACK, P], F32, name="rs", tag=f"bank{m % 2}")
             for t in range(PACK):
@@ -181,23 +202,23 @@ def tile_picked_kqgvarnorm2hopp_none_p_kernel(tc, x_words, x_scales, w1, w2, ga,
 
         def finish_block(m):
             blk = slice(P * m, P * (m + 1))
-            zg = ring.tile([P, PACK * P], BF16, name="zg", align_bytes=64)
+            zg = keep.tile([P, PACK * P], BF16, name="zg", tag=f"zg{m % 2}", align_bytes=64)
             interleaved_product(zg[:], roots[m][:], aga[:, :, blk])
             quantize(zq, zg[:], blk)
             s_ps = psum.tile([P, N], F32, name="s_ps", tag=f"bank{PACK + m}")
             matmul(s_ps, zq, blk, z2q)
             s2 = st[m][:, N:]
             nc.vector.tensor_scalar(s2, s_ps[:], 0.125, None, ALU.mult)
-            g4 = ring.tile([P, N], F32, name="g4")
+            g4 = keep.tile([P, N], F32, name="g4", tag="g4")
             for h in range(2):
                 nc.vector.tensor_copy(g4[:, cols(h)], s2.indirect(half(n4_l, h)))
-            if m < 3:
+            if m < 2:
                 nc.gpsimd.tensor_tensor(st[m][:, :N], s2, g4[:], ALU.add)
             else:
                 nc.vector.scalar_tensor_tensor(st[m][:, :N], s_ps[:], 0.125, g4[:], ALU.mult, ALU.add)
 
         for t in range(2):
-            nc.scalar.activation(babs[t][:], b_ps[t][:], ACT.Abs, scale=gb_sb[:, t : t + 1])
+            nc.scalar.activation(babs[t][:], b_ps[t][:], ACT.Abs)
             fetch_n3(t)
 
         nc.vector.tensor_copy(x_offs[0][:], xw[:].indirect(offs_l[:]))
@@ -237,7 +258,7 @@ def tile_picked_kqgvarnorm2hopp_none_p_kernel(tc, x_words, x_scales, w1, w2, ga,
         for m in range(2, 4):
             for t in range(PACK):
                 members(m, t)
-                if t == 1:
+                if t == [1,1,1][m - 1]:
                     root_a(m - 1)
                     finish_block(m - 1)
         root_a(3)

@@ -18,7 +18,7 @@ PACK = 4
 T = 2048
 N = 512
 HALF = N // 2
-SPARE = 16
+PAD = 192
 FLOPS = 3 * 2 * 512 * 512 * 512
 
 
@@ -40,10 +40,8 @@ def tile_picked_kqgvarnorm2hopp_none_p_kernel(tc, x_words, x_scales, w1, w2, ga,
             nc.sync.dma_start(raw[:], w.rearrange("(p j) c -> p j c", j=PACK))
             return raw
 
-        def load_gain(g, name):
-            t = keep.tile([P, PACK], F32, name=name)
-            nc.sync.dma_start(t[:], g.rearrange("(p t) o -> p (t o)", t=PACK))
-            return t
+        def load_gain(g, rows):
+            nc.sync.dma_start(rows.rearrange("t (b l) -> t b l", l=8), g.rearrange("(b t l) o -> t b (l o)", t=PACK, l=8))
 
         def half(lst, h):
             return lst[:, 16 * h : 16 * (h + 1)]
@@ -54,6 +52,8 @@ def tile_picked_kqgvarnorm2hopp_none_p_kernel(tc, x_words, x_scales, w1, w2, ga,
         warm = keep.tile([P, 2], F32, name="warm")
         nc.gpsimd.memset(warm[:, 0:1], 1.0)
         nc.scalar.activation(warm[:, 1:2], warm[:, 0:1], ACT.Abs_reciprocal_sqrt)
+        gain_rows = keep.tile([P, P], F32, name="gain_rows")
+        nc.gpsimd.memset(gain_rows[:], 0.0)
         xs_rows = keep.tile([P, T // 4], I32, name="xs_rows")
         for q in range(4):
             nc.sync.dma_start(xs_rows[32 * q : 32 * q + 4, :], x_scales[0, 4 * q : 4 * q + 4, :].bitcast(I32))
@@ -63,9 +63,9 @@ def tile_picked_kqgvarnorm2hopp_none_p_kernel(tc, x_words, x_scales, w1, w2, ga,
         xw = keep.tile([P, T], U32, name="xw")
         nc.sync.dma_start(xw[:].bitcast(I32), x_words[0].rearrange("p n t -> p (n t)").bitcast(I32))
         n3_l = load_list(n3, "n3_l")
+        load_gain(gb, gain_rows[0:PACK, :])
+        load_gain(ga, gain_rows[PACK : 2 * PACK, :])
         w1_raw = load_weight(w1, "w1_raw")
-        gb_sb = load_gain(gb, "gb_sb")
-        ga_sb = load_gain(ga, "ga_sb")
         n1_l = load_list(n1, "n1_l")
         n2_l = load_list(n2, "n2_l")
         n4_l = load_list(n4, "n4_l")
@@ -90,18 +90,11 @@ def tile_picked_kqgvarnorm2hopp_none_p_kernel(tc, x_words, x_scales, w1, w2, ga,
             nc.tensor.matmul_mx(out=acc[:], lhsT=lhs[0][:, c].bitcast(FP8X4), lhsT_scale=lhs[1][:, c],
                                 rhs=rhs[0][:].bitcast(FP8X4), rhs_scale=rhs[1][:], start=True, stop=True)
 
-        def cast_weight(shares, raw, grouped):
-            dst = grouped[:].rearrange("p (t m j) -> p m j t", t=PACK, j=PACK)
-            src = raw[:].rearrange("p j (m t) -> p m j t", t=PACK)
-            for copy, ms in shares:
-                copy(dst[:, ms], src[:, ms])
-
-        def safe_inverse(g, name):
-            safe = keep.tile([P, PACK], F32, name=name + "_safe")
-            nc.vector.scalar_tensor_tensor(safe[:], g[:], 0.0, g[:], ALU.is_equal, ALU.add)
-            inv = keep.tile([P, PACK], F32, name=name + "_inv")
-            nc.vector.reciprocal(inv[:], safe[:])
-            return inv
+        def cast_weight(copies, raw, grouped):
+            dst = grouped[:].rearrange("p (t b h i j) -> p t b h j i", t=PACK, h=2, i=4, j=PACK)
+            src = raw[:].rearrange("p j (b t h i) -> p t b h j i", t=PACK, h=2, i=4)
+            for t, copy in enumerate(copies):
+                copy(dst[:, t], src[:, t])
 
         def interleaved_product(dst, in0, in1):
             nc.vector.tensor_tensor(
@@ -128,7 +121,7 @@ def tile_picked_kqgvarnorm2hopp_none_p_kernel(tc, x_words, x_scales, w1, w2, ga,
             nc.vector.tensor_copy(xs[32 * q : 32 * q + 4, :].bitcast(I32), xs_rows[32 * q : 32 * q + 4, :])
         nc.vector.tensor_copy(x_two[1][:], xs[:].indirect(two_l[:]))
         nc.vector.tensor_copy(x_offs[1][:], xs[:].indirect(offs_l[:]))
-        cast_weight([(nc.scalar.copy, slice(0, 96)), (nc.vector.tensor_copy, slice(96, P))], w2_raw, w2g)
+        cast_weight([nc.scalar.copy] * 3 + [nc.vector.tensor_copy], w2_raw, w2g)
         quantize(w2q, w2g[:], whole)
         nc.vector.tensor_copy(x_two[0][:], xw[:].indirect(two_l[:]))
         b_ps = [psum.tile([P, N], F32, name=f"b_ps{t}", tag=f"bank{t}") for t in range(PACK)]
@@ -136,50 +129,50 @@ def tile_picked_kqgvarnorm2hopp_none_p_kernel(tc, x_words, x_scales, w1, w2, ga,
             matmul(b_ps[t], w2q, slice(P * t, P * (t + 1)), x_two)
 
         babs = [keep.tile([P, N], F32, name=f"babs{t}") for t in range(PACK)]
-        bg = [keep.tile([P, N], F32, name=f"bg{t}") for t in range(PACK)]
-        g3 = keep.tile([P, PACK, N], F32, name="g3")
+        bg = [keep.tile([P, 2 * N], F32, name=f"bg{t}") for t in range(PACK)]
         rb = keep.tile([P, PACK, N], F32, name="rb")
         u = keep.tile([P, PACK, N], F32, name="u")
         aga = keep.tile([P, PACK, N], F32, name="aga")
         qs = keep.tile([P, PACK, N], F32, name="qs")
         z2g = keep.tile([P, PACK * N], BF16, name="z2g", align_bytes=64)
-        st = [keep.tile([P, 2 * N], F32, name=f"st{m}") for m in range(4)]
+        st = [keep.tile([P, 2 * N + PAD], F32, name=f"st{m}") for m in range(4)]
+        for m in range(4):
+            nc.gpsimd.memset(st[m][:, 2 * N :], 0.0)
         sums = {}
 
         def scale_b(t):
-            nc.vector.tensor_scalar(bg[t][:], b_ps[t][:], gb_sb[:, t : t + 1], None, ALU.mult)
+            nc.vector.tensor_scalar(bg[t][:, :N], b_ps[t][:], gb_sb[:, t : t + 1], None, ALU.mult)
 
         def fetch_n3(t):
             for h in range(2):
-                nc.scalar.activation(g3[:, t, cols(h)], babs[t][:].indirect(half(n3_l, h)), ACT.Copy)
-            nc.gpsimd.tensor_tensor(asq[t][:, N:], g3[:, t, :], babs[t][:], ALU.add)
+                nc.scalar.activation(bg[t][:, N + HALF * h : N + HALF * (h + 1)], babs[t][:].indirect(half(n3_l, h)), ACT.Copy)
+            nc.gpsimd.tensor_tensor(asq[t][:, N:], bg[t][:, N:], babs[t][:], ALU.add)
 
         def root_b(t):
-            nc.scalar.activation(rb[:, t, :], asq[t][:, N:], ACT.Abs_reciprocal_sqrt, bias=0.5, scale=(1.0 if t < 2 else gb_abs_inv[:, t : t + 1]))
+            nc.scalar.activation(rb[:, t, :], asq[t][:, N:], ACT.Abs_reciprocal_sqrt, bias=0.5)
 
         def fetch_n2(t):
-            for h in range(2):
-                nc.vector.tensor_tensor(u[:, t, cols(h)], bg[t][:].indirect(half(n2_l, h)), rb[:, t, cols(h)], ALU.mult)
+            nc.vector.tensor_tensor(u[:, t, :], bg[t][:].indirect(n2_l[:]), rb[:, t, :], ALU.mult)
 
-        modes = ["pe4","pair","pair","v"]
+        modes = ["mix","mix","mix","mix"]
 
         def members(m, t):
             mode = modes[m]
             if mode == "mix":
-                mode = "pe4" if t < 2 else "pair"
+                mode = "pair" if t in [[],[],[],[]][m] else "pe4"
             if t == 0 and mode != "v":
                 sums[m] = psum.tile([P, PACK, P], F32, name="sums", tag=f"bank{2 + m % 2}")
             if False:
                 g = keep.tile([P, N], F32, name="g", tag=f"zg{m % 2}", align_bytes=64)
             else:
-                g = ring.tile([P, N], F32, name="g", bufs=6)
+                g = ring.tile([P, N], F32, name="g", bufs=3)
             nc.scalar.activation(g[:], asq[t][:].indirect(n1_l[:, 32 * m : 32 * (m + 1)]), ACT.Copy)
             if mode == "v":
                 nc.vector.tensor_reduce(qs[:, t, P * m : P * (m + 1)], g[:].rearrange("p (j r) -> p j r", r=4), mybir.AxisListType.X, ALU.add)
                 return
             gv = g[:].rearrange("p (j r) -> p r j", r=4)
             if mode == "pair":
-                pairs = ring.tile([P, 2, P], F32, name="pairs", bufs=4)
+                pairs = keep.tile([P, 2, P], F32, name="pairs", tag=f"zg{(m - 1) % 2}", align_bytes=64)
                 gj = g[:].rearrange("p (j r) -> p j r", r=4)
                 nc.vector.tensor_tensor(pairs[:].rearrange("p r j -> p j r"), gj[:, :, 0:2], gj[:, :, 2:4], ALU.add)
                 gv = pairs[:]
@@ -207,36 +200,40 @@ def tile_picked_kqgvarnorm2hopp_none_p_kernel(tc, x_words, x_scales, w1, w2, ga,
             quantize(zq, zg[:], blk)
             s_ps = psum.tile([P, N], F32, name="s_ps", tag=f"bank{PACK + m}")
             matmul(s_ps, zq, blk, z2q)
-            s2 = st[m][:, N:]
+            s2 = st[m][:, N : 2 * N]
             nc.vector.tensor_scalar(s2, s_ps[:], 0.125, None, ALU.mult)
             g4 = keep.tile([P, N], F32, name="g4", tag="g4")
-            for h in range(2):
-                nc.vector.tensor_copy(g4[:, cols(h)], s2.indirect(half(n4_l, h)))
-            if m < 2:
+            nc.vector.tensor_copy(g4[:], st[m][:, N:].indirect(n4_l[:]))
+            if m < 3:
                 nc.gpsimd.tensor_tensor(st[m][:, :N], s2, g4[:], ALU.add)
             else:
                 nc.vector.scalar_tensor_tensor(st[m][:, :N], s_ps[:], 0.125, g4[:], ALU.mult, ALU.add)
 
-        for t in range(2):
+        for t in range(3):
             nc.scalar.activation(babs[t][:], b_ps[t][:], ACT.Abs)
             fetch_n3(t)
 
+        gains_ps = psum.tile([P, P], F32, name="gains_ps", tag=f"bank{2 * PACK - 1}")
+        nc.tensor.transpose(gains_ps[:], gain_rows[:], ident[:])
         nc.vector.tensor_copy(x_offs[0][:], xw[:].indirect(offs_l[:]))
-        cast_weight([(nc.vector.tensor_copy, slice(0, P))], w1_raw, w1g)
-        gb_neg = keep.tile([P, PACK], F32, name="gb_neg")
-        nc.vector.tensor_scalar(gb_neg[:], gb_sb[:], -1.0, None, ALU.mult)
+        gains = keep.tile([P, 2 * PACK], F32, name="gains")
+        nc.vector.tensor_copy(gains[:], gains_ps[:, : 2 * PACK])
+        gb_sb, ga_sb = gains[:, :PACK], gains[:, PACK:]
+        cast_weight([nc.vector.tensor_copy] * 4, w1_raw, w1g)
+        safe = keep.tile([P, 2 * PACK], F32, name="safe")
+        nc.vector.scalar_tensor_tensor(safe[:, :PACK], gb_sb, 0.0, gb_sb, ALU.is_equal, ALU.subtract)
+        nc.vector.scalar_tensor_tensor(safe[:, PACK:], ga_sb, 0.0, ga_sb, ALU.is_equal, ALU.add)
         quantize(w1q, w1g[:], whole)
         a_ps = [psum.tile([P, N], F32, name=f"a_ps{t}", tag=f"bank{PACK + t}") for t in range(PACK)]
         for t in range(PACK):
             matmul(a_ps[t], w1q, slice(P * t, P * (t + 1)), x_offs)
-        gb_inv = safe_inverse(gb_sb, "gb")
-        gb_abs_inv = keep.tile([P, PACK], F32, name="gb_abs_inv")
-        nc.vector.scalar_tensor_tensor(gb_abs_inv[:], gb_inv[:], -1.0, gb_inv[:], ALU.mult, ALU.max)
-        ga_inv = safe_inverse(ga_sb, "ga")
+        inv = keep.tile([P, 2 * PACK], F32, name="inv")
+        nc.vector.reciprocal(inv[:], safe[:])
+        gb_neg_inv, ga_inv = inv[:, :PACK], inv[:, PACK:]
 
-        for t in range(2, PACK):
+        for t in range(3, PACK):
             scale_b(t)
-            nc.vector.scalar_tensor_tensor(babs[t][:], b_ps[t][:], gb_neg[:, t : t + 1], bg[t][:], ALU.mult, ALU.max)
+            nc.vector.scalar_tensor_tensor(babs[t][:], bg[t][:, :N], gb_neg_inv[:, t : t + 1], b_ps[t][:], ALU.mult, ALU.max)
             fetch_n3(t)
         for t in range(PACK):
             col = slice(t, t + 1)
@@ -244,7 +241,7 @@ def tile_picked_kqgvarnorm2hopp_none_p_kernel(tc, x_words, x_scales, w1, w2, ga,
             nc.vector.scalar_tensor_tensor(asq[t][:, :N], aga[:, t, :], ga_inv[:, col], a_ps[t][:], ALU.mult, ALU.mult)
             root_b(t)
             members(0, t)
-        for t in range(2):
+        for t in range(3):
             scale_b(t)
         for t in range(PACK):
             fetch_n2(t)

from contextlib import ExitStack

import concourse.mybir as mybir
from concourse.masks import make_identity

F32 = mybir.dt.float32
BF16 = mybir.dt.bfloat16
I32 = mybir.dt.int32
U32 = mybir.dt.uint32
U16 = mybir.dt.uint16
U8 = mybir.dt.uint8
FP8X4 = mybir.dt.float8_e4m3fn_x4
ALU = mybir.AluOpType
ACT = mybir.ActivationFunctionType

P = 128
PACK = 4
T = 2048
N = 512
HALF = N // 2
PAD = 192
FLOPS = 3 * 2 * 512 * 512 * 512


def tile_picked_kqgvarnorm2hopp_none_p_kernel(tc, x_words, x_scales, w1, w2, ga, gb, offs, two, n1, n2, n3, n4, n5, out):
    nc = tc.nc
    with ExitStack() as ctx:
        keep = ctx.enter_context(tc.tile_pool(name="keep", bufs=1))
        ring = ctx.enter_context(tc.tile_pool(name="ring", bufs=2))
        reuse = ctx.enter_context(tc.tile_pool(name="reuse", bufs=1))
        psum = ctx.enter_context(tc.psum_pool(name="psum", bufs=1))

        def load_list(src, name):
            t = keep.tile(list(src.shape), U16, name=name)
            nc.sync.dma_start(t[:], src)
            return t

        def load_weight(w, name):
            raw = keep.tile([P, PACK, N], F32, name=name)
            nc.sync.dma_start(raw[:], w.rearrange("(p j) c -> p j c", j=PACK))
            return raw

        def load_gain(g, rows):
            nc.sync.dma_start(rows.rearrange("t (b l) -> t b l", l=8), g.rearrange("(b t l) o -> t b (l o)", t=PACK, l=8))

        def half(lst, h):
            return lst[:, 16 * h : 16 * (h + 1)]

        def cols(h):
            return slice(HALF * h, HALF * (h + 1))

        warm = keep.tile([P, 2], F32, name="warm")
        nc.gpsimd.memset(warm[:, 0:1], 1.0)
        nc.scalar.activation(warm[:, 1:2], warm[:, 0:1], ACT.Abs_reciprocal_sqrt)
        gain_rows = keep.tile([P, P], F32, name="gain_rows")
        nc.gpsimd.memset(gain_rows[:], 0.0)
        xs_rows = keep.tile([P, T // 4], I32, name="xs_rows")
        for q in range(4):
            nc.sync.dma_start(xs_rows[32 * q : 32 * q + 4, :], x_scales[0, 4 * q : 4 * q + 4, :].bitcast(I32))
        two_l = load_list(two, "two_l")
        offs_l = load_list(offs, "offs_l")
        w2_raw = load_weight(w2, "w2_raw")
        xw = keep.tile([P, T], U32, name="xw")
        nc.sync.dma_start(xw[:].bitcast(I32), x_words[0].rearrange("p n t -> p (n t)").bitcast(I32))
        n3_l = load_list(n3, "n3_l")
        load_gain(gb, gain_rows[0:PACK, :])
        load_gain(ga, gain_rows[PACK : 2 * PACK, :])
        w1_raw = load_weight(w1, "w1_raw")
        n1_l = load_list(n1, "n1_l")
        n2_l = load_list(n2, "n2_l")
        n4_l = load_list(n4, "n4_l")
        n5_l = load_list(n5, "n5_l")

        xs = keep.tile([P, T], U8, name="xs")
        nc.vector.memset(xs[:].bitcast(I32), 0)
        asq = [keep.tile([P, 2 * N], F32, name=f"asq{t}") for t in range(PACK)]
        ident = keep.tile([P, P], F32, name="ident")
        make_identity(nc, ident[:])

        def mx_tiles(name):
            return (
                keep.tile([P, N], U32, name=name + "_codes", align_bytes=64),
                keep.tile([P, N], U8, name=name + "_scales", align_bytes=64),
            )

        def quantize(dst, src, c):
            nc.vector.quantize_mx(out=dst[0][:, c].bitcast(FP8X4), scales=dst[1][:, c], in_=src)

        def matmul(acc, lhs, c, rhs):
            nc.tensor.matmul_mx(out=acc[:], lhsT=lhs[0][:, c].bitcast(FP8X4), lhsT_scale=lhs[1][:, c],
                                rhs=rhs[0][:].bitcast(FP8X4), rhs_scale=rhs[1][:], start=True, stop=True)

        def cast_weight(copies, raw, grouped):
            dst = grouped[:].rearrange("p (t b h i j) -> p t b h j i", t=PACK, h=2, i=4, j=PACK)
            src = raw[:].rearrange("p j (b t h i) -> p t b h j i", t=PACK, h=2, i=4)
            for t, copy in enumerate(copies):
                copy(dst[:, t], src[:, t])

        def interleaved_product(dst, in0, in1):
            nc.vector.tensor_tensor(
                dst.rearrange("p (c i t) -> p c t i", i=2, t=PACK),
                in0.rearrange("p t (c i) -> p c t i", i=2),
                in1.rearrange("p t (c i) -> p c t i", i=2),
                ALU.mult,
            )

        w2g = reuse.tile([P, PACK * N], BF16, name="w2g", align_bytes=64, offset=0)
        w1g = keep.tile([P, PACK * N], BF16, name="w1g", align_bytes=64)
        x_two, x_offs = [
            (
                reuse.tile([P, N], U32, name=name + "_codes", align_bytes=64, offset=4 * N * i),
                keep.tile([P, N], U8, name=name + "_scales", align_bytes=64),
            )
            for i, name in enumerate(("x_two", "x_offs"))
        ]
        w1q, w2q = mx_tiles("w1q"), mx_tiles("w2q")
        zq, z2q = mx_tiles("zq"), mx_tiles("z2q")
        whole = slice(0, N)

        for q in range(4):
            nc.vector.tensor_copy(xs[32 * q : 32 * q + 4, :].bitcast(I32), xs_rows[32 * q : 32 * q + 4, :])
        nc.vector.tensor_copy(x_two[1][:], xs[:].indirect(two_l[:]))
        nc.vector.tensor_copy(x_offs[1][:], xs[:].indirect(offs_l[:]))
        cast_weight([nc.scalar.copy] * 3 + [nc.vector.tensor_copy], w2_raw, w2g)
        quantize(w2q, w2g[:], whole)
        nc.vector.tensor_copy(x_two[0][:], xw[:].indirect(two_l[:]))
        b_ps = [psum.tile([P, N], F32, name=f"b_ps{t}", tag=f"bank{t}") for t in range(PACK)]
        for t in range(PACK):
            matmul(b_ps[t], w2q, slice(P * t, P * (t + 1)), x_two)

        babs = [keep.tile([P, N], F32, name=f"babs{t}") for t in range(PACK)]
        bg = [keep.tile([P, 2 * N], F32, name=f"bg{t}") for t in range(PACK)]
        rb = keep.tile([P, PACK, N], F32, name="rb")
        u = keep.tile([P, PACK, N], F32, name="u")
        aga = keep.tile([P, PACK, N], F32, name="aga")
        qs = keep.tile([P, PACK, N], F32, name="qs")
        z2g = keep.tile([P, PACK * N], BF16, name="z2g", align_bytes=64)
        st = [keep.tile([P, 2 * N + PAD], F32, name=f"st{m}") for m in range(4)]
        for m in range(4):
            nc.gpsimd.memset(st[m][:, 2 * N :], 0.0)
        sums = {}

        def scale_b(t):
            nc.vector.tensor_scalar(bg[t][:, :N], b_ps[t][:], gb_sb[:, t : t + 1], None, ALU.mult)

        def fetch_n3(t):
            for h in range(2):
                nc.scalar.activation(bg[t][:, N + HALF * h : N + HALF * (h + 1)], babs[t][:].indirect(half(n3_l, h)), ACT.Copy)
            nc.gpsimd.tensor_tensor(asq[t][:, N:], bg[t][:, N:], babs[t][:], ALU.add)

        def root_b(t):
            nc.scalar.activation(rb[:, t, :], asq[t][:, N:], ACT.Abs_reciprocal_sqrt, bias=0.5)

        def fetch_n2(t):
            nc.vector.tensor_tensor(u[:, t, :], bg[t][:].indirect(n2_l[:]), rb[:, t, :], ALU.mult)

        modes = ["mix","mix","mix","mix"]

        def members(m, t):
            mode = modes[m]
            if mode == "mix":
                mode = "pair" if t in [[],[],[],[]][m] else "pe4"
            if t == 0 and mode != "v":
                sums[m] = psum.tile([P, PACK, P], F32, name="sums", tag=f"bank{2 + m % 2}")
            if False:
                g = keep.tile([P, N], F32, name="g", tag=f"zg{m % 2}", align_bytes=64)
            else:
                g = ring.tile([P, N], F32, name="g", bufs=3)
            nc.scalar.activation(g[:], asq[t][:].indirect(n1_l[:, 32 * m : 32 * (m + 1)]), ACT.Copy)
            if mode == "v":
                nc.vector.tensor_reduce(qs[:, t, P * m : P * (m + 1)], g[:].rearrange("p (j r) -> p j r", r=4), mybir.AxisListType.X, ALU.add)
                return
            gv = g[:].rearrange("p (j r) -> p r j", r=4)
            if mode == "pair":
                pairs = keep.tile([P, 2, P], F32, name="pairs", tag=f"zg{(m - 1) % 2}", align_bytes=64)
                gj = g[:].rearrange("p (j r) -> p j r", r=4)
                nc.vector.tensor_tensor(pairs[:].rearrange("p r j -> p j r"), gj[:, :, 0:2], gj[:, :, 2:4], ALU.add)
                gv = pairs[:]
            terms = gv.shape[1]
            for r in range(terms):
                nc.tensor.matmul(sums[m][:, t, :], gv[:, r, :], ident[:], start=(r == 0), stop=(r == terms - 1), is_transpose=True)

        roots = {}

        def root_a(m):
            blk = slice(P * m, P * (m + 1))
            if modes[m] == "v":
                roots[m] = keep.tile([P, PACK, P], F32, name="rs_sb")
                nc.scalar.activation(roots[m][:], qs[:, :, blk], ACT.Abs_reciprocal_sqrt, bias=0.5)
                return
            nc.scalar.activation(qs[:, :, blk], sums[m][:], ACT.Abs_reciprocal_sqrt, bias=0.5)
            roots[m] = psum.tile([P, PACK, P], F32, name="rs", tag=f"bank{m % 2}")
            for t in range(PACK):
                nc.tensor.transpose(roots[m][:, t, :], qs[:, t, blk], ident[:])

        def finish_block(m):
            blk = slice(P * m, P * (m + 1))
            zg = keep.tile([P, PACK * P], BF16, name="zg", tag=f"zg{m % 2}", align_bytes=64)
            interleaved_product(zg[:], roots[m][:], aga[:, :, blk])
            quantize(zq, zg[:], blk)
            s_ps = psum.tile([P, N], F32, name="s_ps", tag=f"bank{PACK + m}")
            matmul(s_ps, zq, blk, z2q)
            s2 = st[m][:, N : 2 * N]
            nc.vector.tensor_scalar(s2, s_ps[:], 0.125, None, ALU.mult)
            g4 = keep.tile([P, N], F32, name="g4", tag="g4")
            nc.vector.tensor_copy(g4[:], st[m][:, N:].indirect(n4_l[:]))
            if m < 3:
                nc.gpsimd.tensor_tensor(st[m][:, :N], s2, g4[:], ALU.add)
            else:
                nc.vector.scalar_tensor_tensor(st[m][:, :N], s_ps[:], 0.125, g4[:], ALU.mult, ALU.add)

        for t in range(3):
            nc.scalar.activation(babs[t][:], b_ps[t][:], ACT.Abs)
            fetch_n3(t)

        gains_ps = psum.tile([P, P], F32, name="gains_ps", tag=f"bank{2 * PACK - 1}")
        nc.tensor.transpose(gains_ps[:], gain_rows[:], ident[:])
        nc.vector.tensor_copy(x_offs[0][:], xw[:].indirect(offs_l[:]))
        gains = keep.tile([P, 2 * PACK], F32, name="gains")
        nc.vector.tensor_copy(gains[:], gains_ps[:, : 2 * PACK])
        gb_sb, ga_sb = gains[:, :PACK], gains[:, PACK:]
        cast_weight([nc.vector.tensor_copy] * 4, w1_raw, w1g)
        safe = keep.tile([P, 2 * PACK], F32, name="safe")
        nc.vector.scalar_tensor_tensor(safe[:, :PACK], gb_sb, 0.0, gb_sb, ALU.is_equal, ALU.subtract)
        nc.vector.scalar_tensor_tensor(safe[:, PACK:], ga_sb, 0.0, ga_sb, ALU.is_equal, ALU.add)
        quantize(w1q, w1g[:], whole)
        a_ps = [psum.tile([P, N], F32, name=f"a_ps{t}", tag=f"bank{PACK + t}") for t in range(PACK)]
        for t in range(PACK):
            matmul(a_ps[t], w1q, slice(P * t, P * (t + 1)), x_offs)
        inv = keep.tile([P, 2 * PACK], F32, name="inv")
        nc.vector.reciprocal(inv[:], safe[:])
        gb_neg_inv, ga_inv = inv[:, :PACK], inv[:, PACK:]

        for t in range(3, PACK):
            scale_b(t)
            nc.vector.scalar_tensor_tensor(babs[t][:], bg[t][:, :N], gb_neg_inv[:, t : t + 1], b_ps[t][:], ALU.mult, ALU.max)
            fetch_n3(t)
        for t in range(PACK):
            col = slice(t, t + 1)
            nc.vector.tensor_scalar(aga[:, t, :], a_ps[t][:], ga_sb[:, col], None, ALU.mult)
            nc.vector.scalar_tensor_tensor(asq[t][:, :N], aga[:, t, :], ga_inv[:, col], a_ps[t][:], ALU.mult, ALU.mult)
            root_b(t)
            members(0, t)
        for t in range(3):
            scale_b(t)
        for t in range(PACK):
            fetch_n2(t)
            members(1, t)
            if t == 1:
                root_a(0)
        for h in range(2):
            interleaved_product(z2g[:, PACK * HALF * h : PACK * HALF * (h + 1)], u[:, :, cols(h)], rb[:, :, cols(h)])
        quantize(z2q, z2g[:], whole)
        finish_block(0)
        for m in range(2, 4):
            for t in range(PACK):
                members(m, t)
                if t == [1,1,1][m - 1]:
                    root_a(m - 1)
                    finish_block(m - 1)
        root_a(3)
        finish_block(3)

        for m in range(4):
            for c, lst in ([(cols(h), half(n5_l, h)) for h in range(2)] if m == 3 else [(whole, n5_l[:])]):
                nc.scalar.activation(qs[:, m, c], st[m][:].indirect(lst), ACT.Sigmoid)
                o = ring.tile([P, N], F32, name="o", bufs=5)
                nc.vector.scalar_tensor_tensor(o[:, c], qs[:, m, c], 0.5, st[m][:, c], ALU.subtract, ALU.mult)
                nc.sync.dma_start(out[P * m : P * (m + 1), c], o[:, c])
